import numpy as np
import ml_dtypes


def mxq(x, axis, fmt="e4m3"):
    dtype, down = {"e4m3": (ml_dtypes.float8_e4m3fn, 7), "e5m2": (ml_dtypes.float8_e5m2, 14)}[fmt]
    v = np.moveaxis(np.asarray(x, np.float32).astype(ml_dtypes.bfloat16).astype(np.float64), axis, -1)
    blocks = v.reshape(v.shape[:-1] + (-1, 32))
    amax = np.abs(blocks).max(-1, keepdims=True)
    byte = np.maximum(np.where(amax > 0, np.frexp(amax)[1] - 1 + 127, 0) - down, 1)
    scale = np.exp2(byte - 127.0)
    codes = (blocks / scale).astype(np.float32).astype(dtype).astype(np.float64)
    return np.moveaxis((codes * scale).reshape(v.shape), -1, axis)


WIDE = False


def mx_kscale(k):
    if not WIDE:
        return np.ones(k)
    levels = np.array([10, -10, 5, -5, 0])
    if k % 512:
        return np.exp2(np.random.permutation(np.resize(levels, k // 32))).repeat(32)
    a = np.empty((k // 512, 16))
    for p in range(k // 512):
        a[p, :8] = np.random.permutation(np.resize(levels, 8))
        for g in range(8):
            far = levels[np.abs(levels - a[p, g]) >= 10]
            a[p, g + 8] = far[np.random.randint(len(far))]
    return np.exp2(a.ravel()).repeat(32)


def f64(x):
    return np.asarray(x).astype(np.float64)


def striped8(idx):
    return np.asarray(idx).reshape(8, -1, 16).transpose(0, 2, 1).reshape(128, -1).astype(np.uint16)


def unstriped8(offs):
    return offs.reshape(8, 16, -1).transpose(0, 2, 1).reshape(8, -1).astype(np.int64)


def pick8(x, idx, run):
    r = np.arange(len(x))
    return x[r[:, None], idx[r % (8 * run) // run]]


E2M1 = np.array([0.0, 0.5, 1.0, 1.5, 2.0, 3.0, 4.0, 6.0, -0.0, -0.5, -1.0, -1.5, -2.0, -3.0, -4.0, -6.0])


def pack_weight(w, fmt):
    k, n = w.shape
    w = f64(np.asarray(w, np.float32).astype(ml_dtypes.bfloat16)).reshape(k // 32, 32, n)
    amax = np.abs(w).max(1)
    if fmt == "e4m3":
        byte = np.frexp(amax)[1] - 1 + 127 - 7
    else:
        mant, ex = np.frexp(amax / 6.0)
        byte = np.where(mant > 0.5, ex, ex - 1) + 127
    byte = np.clip(np.where(amax > 0, byte, 1), 1, 254)
    scaled = (w * np.exp2(127.0 - byte)[:, None, :]).reshape(k, n).astype(np.float32)
    by_word = np.ascontiguousarray(scaled.reshape(k // 512, 128, 4, n).transpose(0, 1, 3, 2))
    if fmt == "e4m3":
        words = by_word.astype(ml_dtypes.float8_e4m3fn).view(np.uint8)
    else:
        c = by_word.astype(ml_dtypes.float4_e2m1fn).view(np.uint8) & 0xF
        words = (c[..., 0::2] | (c[..., 1::2] << 4)).reshape(k // 512, 128, 2 * n)
    return np.ascontiguousarray(words), np.ascontiguousarray(byte.astype(np.uint8).reshape(k // 512, 16, n))


def unpack_weight(words, scales, fmt):
    g, _, n = scales.shape
    words = np.ascontiguousarray(words).reshape(g, 128, n, -1)
    if fmt == "e4m3":
        vals = words.view(ml_dtypes.float8_e4m3fn).astype(np.float64)
    else:
        nib = np.empty((g, 128, n, 4), np.uint8)
        nib[..., 0::2] = words & 0xF
        nib[..., 1::2] = words >> 4
        vals = E2M1[nib]
    vals = vals * np.repeat(np.exp2(scales.astype(np.float64) - 127.0), 8, axis=1)[..., None]
    return vals.transpose(0, 1, 3, 2).reshape(g * 512, n)


D, K, T, U, I, Q = 512, 512, 1024, 1024, 512, 128


def setup_inputs():
    n = np.random.standard_normal
    idx = np.stack([np.random.permutation(T)[:I] for _ in range(8)])
    idx2 = np.stack([np.random.permutation(U)[:I] for _ in range(8)])
    idx3 = np.stack([np.random.permutation(T)[:I] for _ in range(8)])
    idx4 = np.stack([np.random.permutation(U)[:I] for _ in range(8)])
    idx5 = np.stack([np.random.permutation(U)[:I] for _ in range(8)])
    idx6 = np.stack([np.random.permutation(T)[:I] for _ in range(8)])
    fd = mx_kscale(D)
    fk = mx_kscale(K)
    wqp = pack_weight(n((D, K)) * 1.0 / np.sqrt(D) * fd[:, None] * fk, "e4m3")
    keysp = pack_weight(n((K, T)) * 1.0 / np.sqrt(K) / fk[:, None], "e2m1")
    notesp = pack_weight(n((D, U)) * 1.0 / np.sqrt(D) * fd[:, None], "e4m3")
    return {
        "states": (n((D, Q)) * 0.95 / fd[:, None]).astype(np.float32),
        "wq_words": wqp[0],
        "wq_scales": wqp[1],
        "keys_words": keysp[0],
        "keys_scales": keysp[1],
        "notes_words": notesp[0],
        "notes_scales": notesp[1],
        "offs": striped8(idx),
        "offs2": striped8(idx2),
        "offs3": striped8(idx3),
        "offs4": striped8(idx4),
        "offs5": striped8(idx5),
        "offs6": striped8(idx6),
    }


def reference(states, wq_words, wq_scales, keys_words, keys_scales, notes_words, notes_scales, offs, offs2, offs3, offs4, offs5, offs6):
    idx = unstriped8(offs)
    idx2 = unstriped8(offs2)
    idx3 = unstriped8(offs3)
    idx4 = unstriped8(offs4)
    idx5 = unstriped8(offs5)
    idx6 = unstriped8(offs6)
    wqu = unpack_weight(wq_words, wq_scales, "e4m3")
    keysu = unpack_weight(keys_words, keys_scales, "e2m1")
    notesu = unpack_weight(notes_words, notes_scales, "e4m3")
    statesq = mxq(f64(states), 0, "e4m3")
    qv = wqu.T @ statesq
    qvq = mxq(qv, 0, "e4m3")
    a = qvq.T @ keysu
    b = statesq.T @ notesu
    f1 = np.zeros((Q, U))
    f1[np.arange(Q)[:, None], idx2[np.arange(Q) % 128 // 16]] = pick8(a, idx, 16)
    f2 = np.zeros((Q, U))
    f2[np.arange(Q)[:, None], idx4[np.arange(Q) % 128 // 16]] = pick8(a, idx3, 16)
    m1 = np.maximum(f1, f2)
    bb = m1 - b
    f3 = np.zeros((Q, T))
    f3[np.arange(Q)[:, None], idx6[np.arange(Q) % 128 // 16]] = pick8(bb, idx5, 16)
    aa = a + f3
    y = pick8(aa, idx, 16)
    return y

@@ -1,0 +1,168 @@
+from contextlib import ExitStack
+
+import concourse.mybir as mybir
+
+D, K, T, U, SLOTS, Q = 512, 512, 1024, 1024, 512, 128
+FLOPS = 2 * D * K * Q + 2 * K * T * Q + 2 * D * U * Q
+
+F32 = mybir.dt.float32
+BF16 = mybir.dt.bfloat16
+I32 = mybir.dt.int32
+U32 = mybir.dt.uint32
+U16 = mybir.dt.uint16
+U8 = mybir.dt.uint8
+FP8X4 = mybir.dt.float8_e4m3fn_x4
+FP4X4 = mybir.dt.float4_e2m1fn_x4
+ALU = mybir.AluOpType
+COPY = mybir.ActivationFunctionType.Copy
+
+P = 128
+PACK = 4
+LIST_COLS = SLOTS // 16
+HALF_SLOTS = SLOTS // 2
+HALF_COLS = LIST_COLS // 2
+A_PIECES = [256, 256, 256, 128, 128]
+BANK = 512
+
+
+def load_scale_rows(queue, plane, rows):
+    for quad in range(4):
+        queue.dma_start(
+            out=plane[32 * quad : 32 * quad + 4, :].bitcast(I32),
+            in_=rows[0, 4 * quad : 4 * quad + 4, :].bitcast(I32),
+        )
+
+
+def tile_attend_twowaves_madeside_kernel(
+    tc, states, wq_words, wq_scales, keys_words, keys_scales, notes_words, notes_scales,
+    offs, offs2, offs3, offs4, offs5, offs6, out,
+):
+    nc = tc.nc
+    with ExitStack() as ctx:
+        sb = ctx.enter_context(tc.tile_pool(name="sb", bufs=1))
+        ps = ctx.enter_context(tc.psum_pool(name="ps", bufs=1))
+
+        lists = [sb.tile([P, LIST_COLS], U16, name="list%d" % n) for n in range(6)]
+        idx, idx2, idx3, idx4, idx5, idx6 = lists
+
+        states_raw = sb.tile([P, PACK, Q], F32, align_bytes=64)
+        wq_raw = sb.tile([P, K], U32, align_bytes=64)
+        wq_plane_raw = sb.tile([P, K], U8, align_bytes=64)
+        keys_codes = sb.tile([P, 2 * T], U8, align_bytes=64)
+        keys_plane = sb.tile([P, T], U8, align_bytes=64)
+        notes_codes = sb.tile([P, U], U32, align_bytes=64)
+        notes_plane = sb.tile([P, U], U8, align_bytes=64)
+        f1 = sb.tile([P, U], F32, align_bytes=64)
+
+        for plane in (wq_plane_raw, keys_plane, notes_plane):
+            nc.gpsimd.memset(plane[:].bitcast(I32), 0)
+        f2 = sb.tile([P, U], F32, align_bytes=64)
+        nc.vector.memset(f1[:], 0.0)
+        nc.vector.memset(f2[:], 0.0)
+
+        nc.sync.dma_start(out=states_raw[:], in_=states.rearrange("(p j) q -> p j q", j=PACK))
+        nc.sync.dma_start(
+            out=wq_raw[:].bitcast(I32), in_=wq_words[0].rearrange("p n t -> p (n t)").bitcast(I32)
+        )
+        load_scale_rows(nc.scalar, wq_plane_raw, wq_scales)
+        nc.sync.dma_start(out=keys_codes[:].bitcast(I32), in_=keys_words[0].bitcast(I32))
+        load_scale_rows(nc.sync, keys_plane, keys_scales)
+        for tile, src in ((idx, offs), (idx3, offs3), (idx2, offs2), (idx4, offs4)):
+            nc.sync.dma_start(tile[:], src)
+        nc.sync.dma_start(
+            out=notes_codes[:].bitcast(I32), in_=notes_words[0].rearrange("p n t -> p (n t)").bitcast(I32)
+        )
+        load_scale_rows(nc.sync, notes_plane, notes_scales)
+        for tile, src in ((idx5, offs5), (idx6, offs6)):
+            nc.sync.dma_start(tile[:], src)
+
+        wq_plane = sb.tile([P, PACK, P], U8, align_bytes=64)
+        nc.vector.tensor_copy(out=wq_plane[:], in_=wq_plane_raw[:].rearrange("p (m t) -> p t m", t=PACK))
+
+        states_bf = sb.tile([P, Q, PACK], BF16, align_bytes=64, tag="states_bf_then_f3")
+        nc.vector.tensor_copy(
+            out=states_bf[:].rearrange("p (c i) j -> p c j i", i=4),
+            in_=states_raw[:].rearrange("p j (c i) -> p c j i", i=4),
+        )
+        states_codes = sb.tile([P, Q], U32, align_bytes=64)
+        states_plane = sb.tile([P, Q], U8, align_bytes=64)
+        nc.vector.quantize_mx(
+            out=states_codes[:].bitcast(FP8X4), scales=states_plane[:],
+            in_=states_bf[:].rearrange("p q j -> p (q j)"),
+        )
+
+        wq_codes = sb.tile([P, PACK, P], U32, align_bytes=64)
+        nc.scalar.copy(
+            out=wq_codes[:].rearrange("p t m -> p m t"),
+            in_=wq_raw[:].rearrange("p (m t) -> p m t", t=PACK),
+        )
+        f3 = sb.tile([P, T], F32, align_bytes=64, tag="states_bf_then_f3")
+        nc.vector.memset(f3[:], 0.0)
+
+        qv_ps = ps.tile([P, PACK, Q], F32, name="qv_ps")
+        for t in range(PACK):
+            nc.tensor.matmul_mx(
+                out=qv_ps[:, t, :], lhsT=wq_codes[:, t, :].bitcast(FP8X4), lhsT_scale=wq_plane[:, t, :],
+                rhs=states_codes[:].bitcast(FP8X4), rhs_scale=states_plane[:], start=True, stop=True,
+            )
+        qv_bf = sb.tile([P, Q, PACK], BF16, align_bytes=64)
+        nc.scalar.copy(out=qv_bf[:], in_=qv_ps[:].rearrange("p t q -> p q t"))
+        qv_codes = sb.tile([P, Q], U32, align_bytes=64)
+        qv_plane = sb.tile([P, Q], U8, align_bytes=64)
+        nc.vector.quantize_mx(
+            out=qv_codes[:].bitcast(FP8X4), scales=qv_plane[:], in_=qv_bf[:].rearrange("p q t -> p (q t)"),
+        )
+        a = sb.tile([P, T], F32, align_bytes=64)
+        for n, width in enumerate(A_PIECES):
+            cols = slice(sum(A_PIECES[:n]), sum(A_PIECES[: n + 1]))
+            a_ps = ps.tile([P, width], F32, name="a_ps%d" % n)
+            nc.tensor.matmul_mx(
+                out=a_ps[:], lhsT=qv_codes[:].bitcast(FP8X4), lhsT_scale=qv_plane[:],
+                rhs=keys_codes[:, 2 * cols.start : 2 * cols.stop].bitcast(FP4X4), rhs_scale=keys_plane[:, cols],
+                start=True, stop=True,
+            )
+            if n % 2 == 0:
+                nc.scalar.copy(out=a[:, cols], in_=a_ps[:])
+            else:
+                nc.vector.tensor_copy(out=a[:, cols], in_=a_ps[:])
+
+        b_ps = []
+        for n in range(U // BANK):
+            cols = slice(n * BANK, (n + 1) * BANK)
+            bank = ps.tile([P, BANK], F32, name="b_ps%d" % n)
+            nc.tensor.matmul_mx(
+                out=bank[:], lhsT=states_codes[:].bitcast(FP8X4), lhsT_scale=states_plane[:],
+                rhs=notes_codes[:, cols].bitcast(FP8X4), rhs_scale=notes_plane[:, cols],
+                start=True, stop=True,
+            )
+            b_ps.append(bank)
+
+        def gather_on_both(dst, window, offsets):
+            nc.vector.tensor_copy(dst[:, :HALF_SLOTS], window[:].indirect(offsets[:, :HALF_COLS]))
+            nc.scalar.activation(dst[:, HALF_SLOTS:], window[:].indirect(offsets[:, HALF_COLS:]), COPY)
+
+        picked1 = sb.tile([P, SLOTS], F32, align_bytes=64)
+        picked3 = sb.tile([P, SLOTS], F32, align_bytes=64)
+        gather_on_both(picked1, a, idx)
+        nc.scalar.activation(picked3[:], a[:].indirect(idx3[:]), COPY)
+        nc.vector.tensor_copy(f1[:].indirect(idx2[:]), picked1[:])
+        nc.vector.tensor_copy(f2[:].indirect(idx4[:]), picked3[:])
+
+        m1 = sb.tile([P, U], F32, align_bytes=64)
+        bb = sb.tile([P, U], F32, align_bytes=64)
+        halves = [slice(n * BANK, (n + 1) * BANK) for n in range(U // BANK)]
+        for cols in halves:
+            nc.vector.tensor_tensor(m1[:, cols], f1[:, cols], f2[:, cols], ALU.max)
+        for cols, bank in zip(halves, b_ps):
+            nc.vector.tensor_tensor(bb[:, cols], m1[:, cols], bank[:], ALU.subtract)
+
+        picked5 = sb.tile([P, SLOTS], F32, align_bytes=64)
+        gather_on_both(picked5, bb, idx5)
+        nc.vector.tensor_copy(f3[:].indirect(idx6[:]), picked5[:])
+
+        aa = sb.tile([P, T], F32, align_bytes=64)
+        nc.vector.tensor_tensor(aa[:], a[:], f3[:], ALU.add)
+        result = sb.tile([P, SLOTS], F32, align_bytes=64)
+        gather_on_both(result, aa, idx)
+        nc.sync.dma_start(out=out[:, :HALF_SLOTS], in_=result[:, :HALF_SLOTS])
+        nc.scalar.dma_start(out=out[:, HALF_SLOTS:], in_=result[:, HALF_SLOTS:])

@@ -47,14 +47,15 @@ def tile_attend_twowaves_madeside_kernel(
 
         states_raw = sb.tile([P, PACK, Q], F32, align_bytes=64)
         wq_raw = sb.tile([P, K], U32, align_bytes=64)
-        wq_plane_raw = sb.tile([P, K], U8, align_bytes=64)
+        early_planes = sb.tile([P, K + T], U8, align_bytes=64)
+        wq_plane_raw = early_planes[:, :K]
+        keys_plane = early_planes[:, K:]
         keys_codes = sb.tile([P, 2 * T], U8, align_bytes=64)
-        keys_plane = sb.tile([P, T], U8, align_bytes=64)
         notes_codes = sb.tile([P, U], U32, align_bytes=64)
         notes_plane = sb.tile([P, U], U8, align_bytes=64)
         f1 = sb.tile([P, U], F32, align_bytes=64)
 
-        for plane in (wq_plane_raw, keys_plane, notes_plane):
+        for plane in (early_planes, notes_plane):
             nc.gpsimd.memset(plane[:].bitcast(I32), 0)
         f2 = sb.tile([P, U], F32, align_bytes=64)
         nc.vector.memset(f1[:], 0.0)
@@ -64,7 +65,7 @@ def tile_attend_twowaves_madeside_kernel(
         nc.sync.dma_start(
             out=wq_raw[:].bitcast(I32), in_=wq_words[0].rearrange("p n t -> p (n t)").bitcast(I32)
         )
-        load_scale_rows(nc.scalar, wq_plane_raw, wq_scales)
+        load_scale_rows(nc.sync, wq_plane_raw, wq_scales)
         nc.sync.dma_start(out=keys_codes[:].bitcast(I32), in_=keys_words[0].bitcast(I32))
         load_scale_rows(nc.sync, keys_plane, keys_scales)
         for tile, src in ((idx, offs), (idx3, offs3), (idx2, offs2), (idx4, offs4)):
@@ -76,10 +77,10 @@ def tile_attend_twowaves_madeside_kernel(
         for tile, src in ((idx5, offs5), (idx6, offs6)):
             nc.sync.dma_start(tile[:], src)
 
-        wq_plane = sb.tile([P, PACK, P], U8, align_bytes=64)
-        nc.vector.tensor_copy(out=wq_plane[:], in_=wq_plane_raw[:].rearrange("p (m t) -> p t m", t=PACK))
+        wq_plane = sb.tile([P, PACK, P], U8, align_bytes=64, tag="wq_plane_then_f3")
+        nc.vector.tensor_copy(out=wq_plane[:], in_=wq_plane_raw.rearrange("p (m t) -> p t m", t=PACK))
 
-        states_bf = sb.tile([P, Q, PACK], BF16, align_bytes=64, tag="states_bf_then_f3")
+        states_bf = sb.tile([P, Q, PACK], BF16, align_bytes=64)
         nc.vector.tensor_copy(
             out=states_bf[:].rearrange("p (c i) j -> p c j i", i=4),
             in_=states_raw[:].rearrange("p j (c i) -> p c j i", i=4),
@@ -96,15 +97,14 @@ def tile_attend_twowaves_madeside_kernel(
             out=wq_codes[:].rearrange("p t m -> p m t"),
             in_=wq_raw[:].rearrange("p (m t) -> p m t", t=PACK),
         )
-        f3 = sb.tile([P, T], F32, align_bytes=64, tag="states_bf_then_f3")
-        nc.vector.memset(f3[:], 0.0)
-
         qv_ps = ps.tile([P, PACK, Q], F32, name="qv_ps")
         for t in range(PACK):
             nc.tensor.matmul_mx(
                 out=qv_ps[:, t, :], lhsT=wq_codes[:, t, :].bitcast(FP8X4), lhsT_scale=wq_plane[:, t, :],
                 rhs=states_codes[:].bitcast(FP8X4), rhs_scale=states_plane[:], start=True, stop=True,
             )
+        f3 = sb.tile([P, T], F32, align_bytes=64, tag="wq_plane_then_f3")
+        nc.vector.memset(f3[:], 0.0)
         qv_bf = sb.tile([P, Q, PACK], BF16, align_bytes=64)
         nc.scalar.copy(out=qv_bf[:], in_=qv_ps[:].rearrange("p t q -> p q t"))
         qv_codes = sb.tile([P, Q], U32, align_bytes=64)
@@ -143,10 +143,15 @@ def tile_attend_twowaves_madeside_kernel(
 
         picked1 = sb.tile([P, SLOTS], F32, align_bytes=64)
         picked3 = sb.tile([P, SLOTS], F32, align_bytes=64)
-        gather_on_both(picked1, a, idx)
-        nc.scalar.activation(picked3[:], a[:].indirect(idx3[:]), COPY)
-        nc.vector.tensor_copy(f1[:].indirect(idx2[:]), picked1[:])
-        nc.vector.tensor_copy(f2[:].indirect(idx4[:]), picked3[:])
+        slot_halves = [slice(0, HALF_SLOTS), slice(HALF_SLOTS, SLOTS)]
+        col_halves = [slice(0, HALF_COLS), slice(HALF_COLS, LIST_COLS)]
+        nc.vector.tensor_copy(picked1[:, slot_halves[0]], a[:].indirect(idx[:, col_halves[0]]))
+        nc.scalar.activation(picked3[:, slot_halves[0]], a[:].indirect(idx3[:, col_halves[0]]), COPY)
+        nc.scalar.activation(picked1[:, slot_halves[1]], a[:].indirect(idx[:, col_halves[1]]), COPY)
+        nc.scalar.activation(picked3[:, slot_halves[1]], a[:].indirect(idx3[:, col_halves[1]]), COPY)
+        for slots, cols in zip(slot_halves, col_halves):
+            nc.vector.tensor_copy(f1[:].indirect(idx2[:, cols]), picked1[:, slots])
+            nc.vector.tensor_copy(f2[:].indirect(idx4[:, cols]), picked3[:, slots])
 
         m1 = sb.tile([P, U], F32, align_bytes=64)
         bb = sb.tile([P, U], F32, align_bytes=64)

@@ -25,8 +25,8 @@ A_PIECES = [256, 256, 256, 128, 128]
 BANK = 512
 
 
-def load_scale_rows(queue, plane, rows):
-    for quad in range(4):
+def load_scale_rows(queues, plane, rows):
+    for quad, queue in enumerate(queues):
         queue.dma_start(
             out=plane[32 * quad : 32 * quad + 4, :].bitcast(I32),
             in_=rows[0, 4 * quad : 4 * quad + 4, :].bitcast(I32),
@@ -47,38 +47,37 @@ def tile_attend_twowaves_madeside_kernel(
 
         states_raw = sb.tile([P, PACK, Q], F32, align_bytes=64)
         wq_raw = sb.tile([P, K], U32, align_bytes=64)
-        early_planes = sb.tile([P, K + T], U8, align_bytes=64)
-        wq_plane_raw = early_planes[:, :K]
-        keys_plane = early_planes[:, K:]
+        wq_plane_raw = sb.tile([P, K], U8, align_bytes=64)
+        keys_plane = sb.tile([P, T], U8, align_bytes=64)
         keys_codes = sb.tile([P, 2 * T], U8, align_bytes=64)
         notes_codes = sb.tile([P, U], U32, align_bytes=64)
         notes_plane = sb.tile([P, U], U8, align_bytes=64)
         f1 = sb.tile([P, U], F32, align_bytes=64)
 
-        for plane in (early_planes, notes_plane):
+        for plane in (wq_plane_raw, keys_plane, notes_plane):
             nc.gpsimd.memset(plane[:].bitcast(I32), 0)
         f2 = sb.tile([P, U], F32, align_bytes=64)
         nc.vector.memset(f1[:], 0.0)
         nc.vector.memset(f2[:], 0.0)
 
         nc.sync.dma_start(out=states_raw[:], in_=states.rearrange("(p j) q -> p j q", j=PACK))
+        load_scale_rows([nc.scalar] * 2 + [nc.sync] * 2, wq_plane_raw, wq_scales)
         nc.sync.dma_start(
             out=wq_raw[:].bitcast(I32), in_=wq_words[0].rearrange("p n t -> p (n t)").bitcast(I32)
         )
-        load_scale_rows(nc.sync, wq_plane_raw, wq_scales)
         nc.sync.dma_start(out=keys_codes[:].bitcast(I32), in_=keys_words[0].bitcast(I32))
-        load_scale_rows(nc.sync, keys_plane, keys_scales)
+        load_scale_rows([nc.sync] * 4, keys_plane, keys_scales)
         for tile, src in ((idx, offs), (idx3, offs3), (idx2, offs2), (idx4, offs4)):
             nc.sync.dma_start(tile[:], src)
         nc.sync.dma_start(
             out=notes_codes[:].bitcast(I32), in_=notes_words[0].rearrange("p n t -> p (n t)").bitcast(I32)
         )
-        load_scale_rows(nc.sync, notes_plane, notes_scales)
+        load_scale_rows([nc.sync] * 4, notes_plane, notes_scales)
         for tile, src in ((idx5, offs5), (idx6, offs6)):
             nc.sync.dma_start(tile[:], src)
 
-        wq_plane = sb.tile([P, PACK, P], U8, align_bytes=64, tag="wq_plane_then_f3")
-        nc.vector.tensor_copy(out=wq_plane[:], in_=wq_plane_raw.rearrange("p (m t) -> p t m", t=PACK))
+        wq_plane = sb.tile([P, PACK, P], U8, align_bytes=64)
+        nc.vector.tensor_copy(out=wq_plane[:], in_=wq_plane_raw[:].rearrange("p (m t) -> p t m", t=PACK))
 
         states_bf = sb.tile([P, Q, PACK], BF16, align_bytes=64)
         nc.vector.tensor_copy(
@@ -93,29 +92,30 @@ def tile_attend_twowaves_madeside_kernel(
         )
 
         wq_codes = sb.tile([P, PACK, P], U32, align_bytes=64)
-        nc.scalar.copy(
-            out=wq_codes[:].rearrange("p t m -> p m t"),
-            in_=wq_raw[:].rearrange("p (m t) -> p m t", t=PACK),
-        )
+        dealt = wq_codes[:].rearrange("p t m -> p m t")
+        as_loaded = wq_raw[:].rearrange("p (m t) -> p m t", t=PACK)
+        nc.scalar.copy(out=dealt[:, : P // 2, :], in_=as_loaded[:, : P // 2, :])
+        nc.vector.tensor_copy(out=dealt[:, P // 2 :, :].bitcast(I32), in_=as_loaded[:, P // 2 :, :].bitcast(I32))
         qv_ps = ps.tile([P, PACK, Q], F32, name="qv_ps")
         for t in range(PACK):
             nc.tensor.matmul_mx(
                 out=qv_ps[:, t, :], lhsT=wq_codes[:, t, :].bitcast(FP8X4), lhsT_scale=wq_plane[:, t, :],
                 rhs=states_codes[:].bitcast(FP8X4), rhs_scale=states_plane[:], start=True, stop=True,
             )
-        f3 = sb.tile([P, T], F32, align_bytes=64, tag="wq_plane_then_f3")
-        nc.vector.memset(f3[:], 0.0)
-        qv_bf = sb.tile([P, Q, PACK], BF16, align_bytes=64)
+        qv_bf = sb.tile([P, Q, PACK], BF16, align_bytes=64, tag="qv_bf_then_f3")
         nc.scalar.copy(out=qv_bf[:], in_=qv_ps[:].rearrange("p t q -> p q t"))
         qv_codes = sb.tile([P, Q], U32, align_bytes=64)
         qv_plane = sb.tile([P, Q], U8, align_bytes=64)
         nc.vector.quantize_mx(
             out=qv_codes[:].bitcast(FP8X4), scales=qv_plane[:], in_=qv_bf[:].rearrange("p q t -> p (q t)"),
         )
+        f3 = sb.tile([P, T], F32, align_bytes=64, tag="qv_bf_then_f3")
+        nc.vector.memset(f3[:], 0.0)
+
         a = sb.tile([P, T], F32, align_bytes=64)
         for n, width in enumerate(A_PIECES):
             cols = slice(sum(A_PIECES[:n]), sum(A_PIECES[: n + 1]))
-            a_ps = ps.tile([P, width], F32, name="a_ps%d" % n)
+            a_ps = ps.tile([P, width], F32, name="a_ps%d" % n, tag="bank%d" % n)
             nc.tensor.matmul_mx(
                 out=a_ps[:], lhsT=qv_codes[:].bitcast(FP8X4), lhsT_scale=qv_plane[:],
                 rhs=keys_codes[:, 2 * cols.start : 2 * cols.stop].bitcast(FP4X4), rhs_scale=keys_plane[:, cols],
@@ -129,7 +129,7 @@ def tile_attend_twowaves_madeside_kernel(
         b_ps = []
         for n in range(U // BANK):
             cols = slice(n * BANK, (n + 1) * BANK)
-            bank = ps.tile([P, BANK], F32, name="b_ps%d" % n)
+            bank = ps.tile([P, BANK], F32, name="b_ps%d" % n, tag="bank%d" % (len(A_PIECES) - U // BANK + n))
             nc.tensor.matmul_mx(
                 out=bank[:], lhsT=states_codes[:].bitcast(FP8X4), lhsT_scale=states_plane[:],
                 rhs=notes_codes[:, cols].bitcast(FP8X4), rhs_scale=notes_plane[:, cols],

from contextlib import ExitStack

import concourse.mybir as mybir

D, K, T, U, SLOTS, Q = 512, 512, 1024, 1024, 512, 128
FLOPS = 2 * D * K * Q + 2 * K * T * Q + 2 * D * U * Q

F32 = mybir.dt.float32
BF16 = mybir.dt.bfloat16
I32 = mybir.dt.int32
U32 = mybir.dt.uint32
U16 = mybir.dt.uint16
U8 = mybir.dt.uint8
FP8X4 = mybir.dt.float8_e4m3fn_x4
FP4X4 = mybir.dt.float4_e2m1fn_x4
ALU = mybir.AluOpType
COPY = mybir.ActivationFunctionType.Copy

P = 128
PACK = 4
LIST_COLS = SLOTS // 16
HALF_SLOTS = SLOTS // 2
HALF_COLS = LIST_COLS // 2
A_PIECES = [256, 256, 256, 128, 128]
BANK = 512


def load_scale_rows(queues, plane, rows):
    for quad, queue in enumerate(queues):
        queue.dma_start(
            out=plane[32 * quad : 32 * quad + 4, :].bitcast(I32),
            in_=rows[0, 4 * quad : 4 * quad + 4, :].bitcast(I32),
        )


def tile_attend_twowaves_madeside_kernel(
    tc, states, wq_words, wq_scales, keys_words, keys_scales, notes_words, notes_scales,
    offs, offs2, offs3, offs4, offs5, offs6, out,
):
    nc = tc.nc
    with ExitStack() as ctx:
        sb = ctx.enter_context(tc.tile_pool(name="sb", bufs=1))
        ps = ctx.enter_context(tc.psum_pool(name="ps", bufs=1))

        lists = [sb.tile([P, LIST_COLS], U16, name="list%d" % n) for n in range(6)]
        idx, idx2, idx3, idx4, idx5, idx6 = lists

        states_raw = sb.tile([P, PACK, Q], F32, align_bytes=64)
        wq_raw = sb.tile([P, K], U32, align_bytes=64)
        wq_plane_raw = sb.tile([P, K], U8, align_bytes=64)
        keys_plane = sb.tile([P, T], U8, align_bytes=64)
        keys_codes = sb.tile([P, 2 * T], U8, align_bytes=64)
        notes_codes = sb.tile([P, U], U32, align_bytes=64)
        notes_plane = sb.tile([P, U], U8, align_bytes=64)
        f1 = sb.tile([P, U], F32, align_bytes=64)

        for plane in (wq_plane_raw, keys_plane, notes_plane):
            nc.gpsimd.memset(plane[:].bitcast(I32), 0)
        f2 = sb.tile([P, U], F32, align_bytes=64)
        nc.vector.memset(f1[:], 0.0)
        nc.vector.memset(f2[:], 0.0)

        nc.sync.dma_start(out=states_raw[:], in_=states.rearrange("(p j) q -> p j q", j=PACK))
        load_scale_rows([nc.scalar] * 2 + [nc.sync] * 2, wq_plane_raw, wq_scales)
        nc.sync.dma_start(
            out=wq_raw[:].bitcast(I32), in_=wq_words[0].rearrange("p n t -> p (n t)").bitcast(I32)
        )
        nc.sync.dma_start(out=keys_codes[:].bitcast(I32), in_=keys_words[0].bitcast(I32))
        load_scale_rows([nc.sync] * 4, keys_plane, keys_scales)
        for tile, src in ((idx, offs), (idx3, offs3), (idx2, offs2), (idx4, offs4)):
            nc.sync.dma_start(tile[:], src)
        nc.sync.dma_start(
            out=notes_codes[:].bitcast(I32), in_=notes_words[0].rearrange("p n t -> p (n t)").bitcast(I32)
        )
        load_scale_rows([nc.sync] * 4, notes_plane, notes_scales)
        for tile, src in ((idx5, offs5), (idx6, offs6)):
            nc.sync.dma_start(tile[:], src)

        wq_plane = sb.tile([P, PACK, P], U8, align_bytes=64)
        nc.vector.tensor_copy(out=wq_plane[:], in_=wq_plane_raw[:].rearrange("p (m t) -> p t m", t=PACK))

        states_bf = sb.tile([P, Q, PACK], BF16, align_bytes=64)
        nc.vector.tensor_copy(
            out=states_bf[:].rearrange("p (c i) j -> p c j i", i=4),
            in_=states_raw[:].rearrange("p j (c i) -> p c j i", i=4),
        )
        states_codes = sb.tile([P, Q], U32, align_bytes=64)
        states_plane = sb.tile([P, Q], U8, align_bytes=64)
        nc.vector.quantize_mx(
            out=states_codes[:].bitcast(FP8X4), scales=states_plane[:],
            in_=states_bf[:].rearrange("p q j -> p (q j)"),
        )

        wq_codes = sb.tile([P, PACK, P], U32, align_bytes=64)
        dealt = wq_codes[:].rearrange("p t m -> p m t")
        as_loaded = wq_raw[:].rearrange("p (m t) -> p m t", t=PACK)
        nc.scalar.copy(out=dealt[:, : P // 2, :], in_=as_loaded[:, : P // 2, :])
        nc.vector.tensor_copy(out=dealt[:, P // 2 :, :].bitcast(I32), in_=as_loaded[:, P // 2 :, :].bitcast(I32))
        qv_ps = ps.tile([P, PACK, Q], F32, name="qv_ps")
        for t in range(PACK):
            nc.tensor.matmul_mx(
                out=qv_ps[:, t, :], lhsT=wq_codes[:, t, :].bitcast(FP8X4), lhsT_scale=wq_plane[:, t, :],
                rhs=states_codes[:].bitcast(FP8X4), rhs_scale=states_plane[:], start=True, stop=True,
            )
        qv_bf = sb.tile([P, Q, PACK], BF16, align_bytes=64, tag="qv_bf_then_f3")
        nc.scalar.copy(out=qv_bf[:], in_=qv_ps[:].rearrange("p t q -> p q t"))
        qv_codes = sb.tile([P, Q], U32, align_bytes=64)
        qv_plane = sb.tile([P, Q], U8, align_bytes=64)
        nc.vector.quantize_mx(
            out=qv_codes[:].bitcast(FP8X4), scales=qv_plane[:], in_=qv_bf[:].rearrange("p q t -> p (q t)"),
        )
        f3 = sb.tile([P, T], F32, align_bytes=64, tag="qv_bf_then_f3")
        nc.vector.memset(f3[:], 0.0)

        a = sb.tile([P, T], F32, align_bytes=64)
        for n, width in enumerate(A_PIECES):
            cols = slice(sum(A_PIECES[:n]), sum(A_PIECES[: n + 1]))
            a_ps = ps.tile([P, width], F32, name="a_ps%d" % n, tag="bank%d" % n)
            nc.tensor.matmul_mx(
                out=a_ps[:], lhsT=qv_codes[:].bitcast(FP8X4), lhsT_scale=qv_plane[:],
                rhs=keys_codes[:, 2 * cols.start : 2 * cols.stop].bitcast(FP4X4), rhs_scale=keys_plane[:, cols],
                start=True, stop=True,
            )
            if n % 2 == 0:
                nc.scalar.copy(out=a[:, cols], in_=a_ps[:])
            else:
                nc.vector.tensor_copy(out=a[:, cols], in_=a_ps[:])

        b_ps = []
        for n in range(U // BANK):
            cols = slice(n * BANK, (n + 1) * BANK)
            bank = ps.tile([P, BANK], F32, name="b_ps%d" % n, tag="bank%d" % (len(A_PIECES) - U // BANK + n))
            nc.tensor.matmul_mx(
                out=bank[:], lhsT=states_codes[:].bitcast(FP8X4), lhsT_scale=states_plane[:],
                rhs=notes_codes[:, cols].bitcast(FP8X4), rhs_scale=notes_plane[:, cols],
                start=True, stop=True,
            )
            b_ps.append(bank)

        def gather_on_both(dst, window, offsets):
            nc.vector.tensor_copy(dst[:, :HALF_SLOTS], window[:].indirect(offsets[:, :HALF_COLS]))
            nc.scalar.activation(dst[:, HALF_SLOTS:], window[:].indirect(offsets[:, HALF_COLS:]), COPY)

        picked1 = sb.tile([P, SLOTS], F32, align_bytes=64)
        picked3 = sb.tile([P, SLOTS], F32, align_bytes=64)
        slot_halves = [slice(0, HALF_SLOTS), slice(HALF_SLOTS, SLOTS)]
        col_halves = [slice(0, HALF_COLS), slice(HALF_COLS, LIST_COLS)]
        nc.vector.tensor_copy(picked1[:, slot_halves[0]], a[:].indirect(idx[:, col_halves[0]]))
        nc.scalar.activation(picked3[:, slot_halves[0]], a[:].indirect(idx3[:, col_halves[0]]), COPY)
        nc.scalar.activation(picked1[:, slot_halves[1]], a[:].indirect(idx[:, col_halves[1]]), COPY)
        nc.scalar.activation(picked3[:, slot_halves[1]], a[:].indirect(idx3[:, col_halves[1]]), COPY)
        for slots, cols in zip(slot_halves, col_halves):
            nc.vector.tensor_copy(f1[:].indirect(idx2[:, cols]), picked1[:, slots])
            nc.vector.tensor_copy(f2[:].indirect(idx4[:, cols]), picked3[:, slots])

        m1 = sb.tile([P, U], F32, align_bytes=64)
        bb = sb.tile([P, U], F32, align_bytes=64)
        halves = [slice(n * BANK, (n + 1) * BANK) for n in range(U // BANK)]
        for cols in halves:
            nc.vector.tensor_tensor(m1[:, cols], f1[:, cols], f2[:, cols], ALU.max)
        for cols, bank in zip(halves, b_ps):
            nc.vector.tensor_tensor(bb[:, cols], m1[:, cols], bank[:], ALU.subtract)

        picked5 = sb.tile([P, SLOTS], F32, align_bytes=64)
        gather_on_both(picked5, bb, idx5)
        nc.vector.tensor_copy(f3[:].indirect(idx6[:]), picked5[:])

        aa = sb.tile([P, T], F32, align_bytes=64)
        nc.vector.tensor_tensor(aa[:], a[:], f3[:], ALU.add)
        result = sb.tile([P, SLOTS], F32, align_bytes=64)
        gather_on_both(result, aa, idx)
        nc.sync.dma_start(out=out[:, :HALF_SLOTS], in_=result[:, :HALF_SLOTS])
        nc.scalar.dma_start(out=out[:, HALF_SLOTS:], in_=result[:, HALF_SLOTS:])
